import numpy as np
import ml_dtypes


def mxq(x, axis, fmt="e4m3"):
    dtype, down = {"e4m3": (ml_dtypes.float8_e4m3fn, 7), "e5m2": (ml_dtypes.float8_e5m2, 14)}[fmt]
    v = np.moveaxis(np.asarray(x, np.float32).astype(ml_dtypes.bfloat16).astype(np.float64), axis, -1)
    blocks = v.reshape(v.shape[:-1] + (-1, 32))
    amax = np.abs(blocks).max(-1, keepdims=True)
    byte = np.maximum(np.where(amax > 0, np.frexp(amax)[1] - 1 + 127, 0) - down, 1)
    scale = np.exp2(byte - 127.0)
    codes = (blocks / scale).astype(np.float32).astype(dtype).astype(np.float64)
    return np.moveaxis((codes * scale).reshape(v.shape), -1, axis)


WIDE = False


def mx_kscale(k):
    if not WIDE:
        return np.ones(k)
    levels = np.array([10, -10, 5, -5, 0])
    if k % 512:
        return np.exp2(np.random.permutation(np.resize(levels, k // 32))).repeat(32)
    a = np.empty((k // 512, 16))
    for p in range(k // 512):
        a[p, :8] = np.random.permutation(np.resize(levels, 8))
        for g in range(8):
            far = levels[np.abs(levels - a[p, g]) >= 10]
            a[p, g + 8] = far[np.random.randint(len(far))]
    return np.exp2(a.ravel()).repeat(32)


def f64(x):
    return np.asarray(x).astype(np.float64)


def striped(idx):
    return np.tile(idx.reshape(-1, 16).T, (8, 1)).astype(np.uint16)


def unstriped(offs):
    return offs[:16].T.reshape(-1).astype(np.int64)


E2M1 = np.array([0.0, 0.5, 1.0, 1.5, 2.0, 3.0, 4.0, 6.0, -0.0, -0.5, -1.0, -1.5, -2.0, -3.0, -4.0, -6.0])


def pack_weight(w, fmt):
    k, n = w.shape
    w = f64(np.asarray(w, np.float32).astype(ml_dtypes.bfloat16)).reshape(k // 32, 32, n)
    amax = np.abs(w).max(1)
    if fmt == "e4m3":
        byte = np.frexp(amax)[1] - 1 + 127 - 7
    else:
        mant, ex = np.frexp(amax / 6.0)
        byte = np.where(mant > 0.5, ex, ex - 1) + 127
    byte = np.clip(np.where(amax > 0, byte, 1), 1, 254)
    scaled = (w * np.exp2(127.0 - byte)[:, None, :]).reshape(k, n).astype(np.float32)
    by_word = np.ascontiguousarray(scaled.reshape(k // 512, 128, 4, n).transpose(0, 1, 3, 2))
    if fmt == "e4m3":
        words = by_word.astype(ml_dtypes.float8_e4m3fn).view(np.uint8)
    else:
        c = by_word.astype(ml_dtypes.float4_e2m1fn).view(np.uint8) & 0xF
        words = (c[..., 0::2] | (c[..., 1::2] << 4)).reshape(k // 512, 128, 2 * n)
    return np.ascontiguousarray(words), np.ascontiguousarray(byte.astype(np.uint8).reshape(k // 512, 16, n))


def unpack_weight(words, scales, fmt):
    g, _, n = scales.shape
    words = np.ascontiguousarray(words).reshape(g, 128, n, -1)
    if fmt == "e4m3":
        vals = words.view(ml_dtypes.float8_e4m3fn).astype(np.float64)
    else:
        nib = np.empty((g, 128, n, 4), np.uint8)
        nib[..., 0::2] = words & 0xF
        nib[..., 1::2] = words >> 4
        vals = E2M1[nib]
    vals = vals * np.repeat(np.exp2(scales.astype(np.float64) - 127.0), 8, axis=1)[..., None]
    return vals.transpose(0, 1, 3, 2).reshape(g * 512, n)


def gelu(v):
    return 0.5 * v * (1.0 + np.tanh(np.sqrt(2.0 / np.pi) * (v + 0.044715 * v**3)))


K, H, T, S, T3, S2, T2, P = 1536, 1024, 2048, 512, 2048, 512, 1024, 512


def setup_inputs():
    n = np.random.standard_normal
    s = mx_kscale(K)[:, None]
    u = mx_kscale(H)[:, None]
    tab_words, tab_scales = pack_weight(n((K, T)) * s, "e4m3")
    tab2_words, tab2_scales = pack_weight(n((H, T3)) / np.sqrt(H) / u, "e4m3")
    w4_words, w4_scales = pack_weight(n((H, S2)) / np.sqrt(H) / u, "e2m1")
    return {
        "tab_words": tab_words, "tab_scales": tab_scales,
        "offs": striped(np.random.permutation(T)[:S]),
        "w1": (2.0 * n((K, H)) / np.sqrt(K) / s).astype(np.float32),
        "gain": (np.exp(0.3 * n(H)) * u[:, 0]).astype(np.float32),
        "page0": (n((H, T2)) * u).astype(np.float32),
        "wgs": np.exp(0.3 * n((128, S))).astype(np.float32),
        "offs3": striped(np.random.permutation(T2)[:S]),
        "tab2_words": tab2_words, "tab2_scales": tab2_scales,
        "offs2": striped(np.random.permutation(T3)[:S2]),
        "gm": n((H, T2)).astype(np.float32),
        "w4_words": w4_words, "w4_scales": w4_scales,
        "pos1": striped(np.random.permutation(T2)[:P]),
        "pos2": striped(np.random.permutation(T2)[:P]),
        "level": n(S2).astype(np.float32),
    }


def reference(tab_words, tab_scales, offs, w1, gain, page0, wgs, offs3, tab2_words, tab2_scales, offs2,
              gm, w4_words, w4_scales, pos1, pos2, level):
    v = unpack_weight(tab_words, tab_scales, "e4m3")[:, unstriped(offs)]
    v2 = unpack_weight(tab2_words, tab2_scales, "e4m3")[:, unstriped(offs2)]
    w4 = unpack_weight(w4_words, w4_scales, "e2m1")
    d = mxq(f64(w1), 0, "e4m3").T @ v
    h = np.sqrt(np.abs(d)) * f64(gain)[:, None]
    page = f64(page0).copy()
    page[:, unstriped(offs3)] = np.tile(f64(wgs), (H // 128, 1)) * h
    x = page * f64(gm)
    e = v2.T @ mxq(page, 0, "e4m3") + w4.T @ mxq(x, 0, "e4m3")
    return np.maximum(e[:, unstriped(pos1)], e[:, unstriped(pos2)]) - f64(level)[:, None]

@@ -1,0 +1,276 @@
+from contextlib import ExitStack
+
+import concourse.mybir as mybir
+
+K, H, T, S, T2, M = 1536, 1024, 2048, 512, 1024, 512
+FLOPS = 2 * K * H * S + 2 * 2 * H * M * T2
+
+F32 = mybir.dt.float32
+BF16 = mybir.dt.bfloat16
+I32 = mybir.dt.int32
+U32 = mybir.dt.uint32
+U16 = mybir.dt.uint16
+U8 = mybir.dt.uint8
+FP8X4 = mybir.dt.float8_e4m3fn_x4
+FP4X4 = mybir.dt.float4_e2m1fn_x4
+ACT = mybir.ActivationFunctionType
+ALU = mybir.AluOpType
+
+P = 128
+PACK = 4
+PASS = P * PACK
+K_PASSES = K // PASS
+R_PASSES = H // PASS
+HALF = 512
+HALVES = T2 // HALF
+M_TILES = M // P
+
+
+def tile_list_mangrove_stand_scores_kernel(
+    tc, tab_words, tab_scales, offs, w1, gain, page0, wgs, offs3, tab2_words, tab2_scales, offs2,
+    gm, w4_words, w4_scales, pos1, pos2, level, out,
+):
+    nc = tc.nc
+    with ExitStack() as ctx:
+        lists = ctx.enter_context(tc.tile_pool(name="lists", bufs=1))
+        keep = ctx.enter_context(tc.tile_pool(name="keep", bufs=1))
+        ring = ctx.enter_context(tc.tile_pool(name="ring", bufs=2))
+        psum = ctx.enter_context(tc.psum_pool(name="psum", bufs=1))
+
+        def load_list(name, src):
+            tile = lists.tile([P, S // 16], U16, name=name)
+            nc.sync.dma_start(tile[:], src)
+            return tile
+
+        def load_scale_rows(plane, src, passes):
+            for q in range(4):
+                nc.sync.dma_start(
+                    plane[32 * q : 32 * q + 4 * passes, :].bitcast(I32),
+                    src[:, 4 * q : 4 * q + 4, :].bitcast(I32),
+                )
+
+        def load_table_words(src, a, name, tag):
+            words = keep.tile([P, T], U32, name=name, tag=tag, align_bytes=64)
+            nc.sync.dma_start(words[:].bitcast(I32), src[a].rearrange("p n i -> p (n i)").bitcast(I32))
+            return words
+
+        def load_w1(b, a):
+            raw = keep.tile([P, PACK, PASS], F32, name=f"w1_raw{b}{a}", tag=f"w1_slot{a}", align_bytes=64)
+            src = w1[a * PASS : (a + 1) * PASS, b * PASS : (b + 1) * PASS]
+            nc.sync.dma_start(raw[:], src.rearrange("(p j) c -> p j c", j=PACK))
+            return raw
+
+        def load_page(b, t):
+            tile = keep.tile([P, T2], F32, name=f"page{b}{t}", tag=f"page_slot{b}{t}", align_bytes=64)
+            nc.sync.dma_start(tile[:], page0.rearrange("(b p t) n -> b t p n", b=R_PASSES, t=PACK)[b, t])
+            return tile
+
+        def load_gm(b, half, tag):
+            tile = keep.tile([P, PACK, HALF], F32, name=f"gm{b}{half}", tag=tag, align_bytes=64)
+            src = gm[b * PASS : (b + 1) * PASS, half * HALF : (half + 1) * HALF]
+            nc.sync.dma_start(tile[:], src.rearrange("(p t) n -> p t n", t=PACK))
+            return tile
+
+        def gather(name, window, offsets, dtype):
+            picked = keep.tile([P, S], dtype, name=name, align_bytes=64)
+            nc.vector.tensor_copy(picked[:], window[:].indirect(offsets[:]))
+            return picked
+
+        def quantise(name, grouped):
+            codes = keep.tile([P, HALF], U32, name=name + "_codes", align_bytes=64)
+            scales = keep.tile([P, HALF], U8, name=name + "_scales", align_bytes=64)
+            nc.vector.quantize_mx(out=codes[:].bitcast(FP8X4), scales=scales[:], in_=grouped[:])
+            return codes, scales
+
+        def group_w1(raw):
+            grouped = ring.tile([P, PACK * PASS], BF16, name="w1_grouped", align_bytes=64)
+            nc.scalar.copy(
+                grouped[:].rearrange("p (t m j) -> p m j t", t=PACK, j=PACK),
+                raw[:].rearrange("p j (m t) -> p m j t", t=PACK),
+            )
+            return grouped
+
+        def bank(i, name):
+            return psum.tile([P, HALF], F32, name=name, tag=f"bank{i}")
+
+        v_plane = keep.tile([P, T], U8, name="v_plane", align_bytes=64)
+        v2_plane = keep.tile([P, T], U8, name="v2_plane", align_bytes=64)
+        w4_plane = keep.tile([P, R_PASSES, M], U8, name="w4_plane", align_bytes=64)
+        for plane in (v_plane, v2_plane, w4_plane):
+            nc.vector.memset(plane[:].bitcast(I32), 0)
+
+        idx = load_list("idx", offs)
+        w1_raw, v_words, page, gm_sb = {}, {}, {}, {}
+        for a in range(K_PASSES):
+            w1_raw[0, a] = load_w1(0, a)
+            if a == 0:
+                load_scale_rows(v_plane, tab_scales, K_PASSES)
+            v_words[a] = load_table_words(tab_words, a, f"v_words{a}", f"tab_slot{a}")
+        gain_sb = keep.tile([P, R_PASSES, PACK], F32, name="gain_sb")
+        nc.sync.dma_start(gain_sb[:], gain.rearrange("(b p t) -> p b t", b=R_PASSES, t=PACK))
+        idx3 = load_list("idx3", offs3)
+        wgs_sb = keep.tile([P, PACK, S], F32, name="wgs_sb", align_bytes=64)
+        for q in (0, 2, 1, 3):
+            nc.sync.dma_start(wgs_sb[32 * q : 32 * q + 32, :, :], wgs.rearrange("(q t) j -> q t j", t=PACK))
+        page[0, 0] = load_page(0, 0)
+        page[0, 1] = load_page(0, 1)
+
+        v_scales = gather("v_scales", v_plane, idx, U8)
+        v_codes, w1_q = {}, {}
+        for a in range(K_PASSES):
+            w1_q[0, a] = quantise(f"w1_0{a}", group_w1(w1_raw[0, a]))
+            v_codes[a] = gather(f"v_codes{a}", v_words[a], idx, U32)
+
+        w1_raw[1, 0] = load_w1(1, 0)
+        w1_raw[1, 1] = load_w1(1, 1)
+        page[0, 2] = load_page(0, 2)
+        w1_raw[1, 2] = load_w1(1, 2)
+        page[0, 3] = load_page(0, 3)
+        for half in range(HALVES):
+            gm_sb[0, half] = load_gm(0, half, f"gm_slot{half}")
+        for t in range(PACK):
+            page[1, t] = load_page(1, t)
+        for half in range(HALVES):
+            gm_sb[1, half] = load_gm(1, half, f"tab_slot{half}")
+        idx2 = load_list("idx2", offs2)
+        p1 = load_list("p1", pos1)
+        p2 = load_list("p2", pos2)
+        w4_sb = keep.tile([P, R_PASSES, 2 * M], U8, name="w4_sb", align_bytes=64)
+        nc.sync.dma_start(w4_sb[:].bitcast(I32), w4_words.rearrange("a p c -> p a c").bitcast(I32))
+        load_scale_rows(v2_plane, tab2_scales, R_PASSES)
+        for q in range(4):
+            nc.sync.dma_start(
+                w4_plane[32 * q : 32 * q + 4, :, :].bitcast(I32),
+                w4_scales[:, 4 * q : 4 * q + 4, :].rearrange("a r c -> r a c").bitcast(I32),
+            )
+
+        def first_stage(b):
+            sums = []
+            for t in range(PACK):
+                d = bank(PACK * b + t, f"d{b}{t}")
+                cols = slice(t * P, (t + 1) * P)
+                for a in range(K_PASSES):
+                    codes, scales = w1_q[b, a]
+                    nc.tensor.matmul_mx(
+                        out=d[:],
+                        lhsT=codes[:, cols].bitcast(FP8X4), lhsT_scale=scales[:, cols],
+                        rhs=v_codes[a][:].bitcast(FP8X4), rhs_scale=v_scales[4 * a :, :],
+                        start=(a == 0), stop=(a == K_PASSES - 1),
+                    )
+                sums.append(d)
+            return sums
+
+        def features(d, b, t):
+            root = ring.tile([P, S], F32, name="root")
+            nc.scalar.activation(root[:], d[:], ACT.Abs)
+            nc.scalar.activation(root[:], root[:], ACT.Sqrt)
+            h = ring.tile([P, S], F32, name="h", bufs=3)
+            nc.scalar.activation(h[:], root[:], ACT.Copy, scale=gain_sb[:, b, t : t + 1])
+            return h
+
+        def scatter(h, b, t):
+            nc.vector.tensor_tensor(page[b, t][:].indirect(idx3[:]), h[:], wgs_sb[:, t, :], ALU.mult)
+
+        joined = [keep.tile([P, PACK, T2], F32, name=f"joined{b}", align_bytes=64) for b in range(R_PASSES)]
+
+        def join(b, t):
+            nc.scalar.copy(joined[b][:, t, :], page[b, t][:])
+
+        def walk_rows(ap):
+            return ap.rearrange("p t (c i) -> p c t i", i=4)
+
+        def walk_words(ap):
+            return ap.rearrange("p (c i t) -> p c t i", i=4, t=PACK)
+
+        page_q, x_q = {}, {}
+
+        def second_stage_operands(b):
+            grouped = {}
+            for half in range(HALVES):
+                rows = walk_rows(joined[b][:, :, half * HALF : (half + 1) * HALF])
+                x_grouped = ring.tile([P, PACK * HALF], BF16, name="x_grouped", align_bytes=64)
+                nc.vector.tensor_tensor(walk_words(x_grouped[:]), rows, walk_rows(gm_sb[b, half][:]), ALU.mult)
+                page_grouped = ring.tile([P, PACK * HALF], BF16, name="page_grouped", align_bytes=64)
+                nc.scalar.activation(walk_words(page_grouped[:]), rows, ACT.Copy)
+                grouped[half] = (x_grouped, page_grouped)
+            for half in range(HALVES):
+                x_q[b, half] = quantise(f"x{b}{half}", grouped[half][0])
+            for half in range(HALVES):
+                page_q[b, half] = quantise(f"page_q{b}{half}", grouped[half][1])
+
+        d0 = first_stage(0)
+        h = {(0, 0): features(d0[0], 0, 0), (0, 1): features(d0[1], 0, 1)}
+        scatter(h[0, 0], 0, 0)
+        h[0, 2] = features(d0[2], 0, 2)
+        join(0, 0)
+        scatter(h[0, 1], 0, 1)
+        h[0, 3] = features(d0[3], 0, 3)
+        w1_q[1, 0] = quantise("w1_10", group_w1(w1_raw[1, 0]))
+        join(0, 1)
+        scatter(h[0, 2], 0, 2)
+        w1_q[1, 1] = quantise("w1_11", group_w1(w1_raw[1, 1]))
+        w1_q[1, 2] = quantise("w1_12", group_w1(w1_raw[1, 2]))
+        join(0, 2)
+        scatter(h[0, 3], 0, 3)
+        join(0, 3)
+        v2_words = [load_table_words(tab2_words, b, f"v2_words{b}", f"w1_slot{b}") for b in range(R_PASSES)]
+        level_sb = keep.tile([P, M_TILES], F32, name="level_sb")
+        with nc.allow_non_contiguous_dma(reason="one level for each partition and tile of rows"):
+            nc.sync.dma_start(level_sb[:], level.rearrange("(m p) -> p m", p=P))
+        d1 = first_stage(1)
+        h[1, 0] = features(d1[0], 1, 0)
+        h[1, 1] = features(d1[1], 1, 1)
+        second_stage_operands(0)
+        scatter(h[1, 0], 1, 0)
+        h[1, 2] = features(d1[2], 1, 2)
+        join(1, 0)
+        scatter(h[1, 1], 1, 1)
+        h[1, 3] = features(d1[3], 1, 3)
+        join(1, 1)
+        scatter(h[1, 2], 1, 2)
+        join(1, 2)
+        scatter(h[1, 3], 1, 3)
+        join(1, 3)
+        v2_scales = gather("v2_scales", v2_plane, idx2, U8)
+        v2_codes = [gather(f"v2_codes{b}", v2_words[b], idx2, U32) for b in range(R_PASSES)]
+        second_stage_operands(1)
+
+        neg_level = keep.tile([P, M_TILES], F32, name="neg_level")
+        nc.scalar.activation(neg_level[:], level_sb[:], ACT.Copy, scale=-1.0)
+
+        e_banks = {(m, half): bank(HALVES * m + half, f"e{m}{half}") for m in range(M_TILES) for half in range(HALVES)}
+        for b in range(R_PASSES):
+            for product in range(2):
+                for m in range(M_TILES):
+                    cols = slice(m * P, (m + 1) * P)
+                    for half in range(HALVES):
+                        if product == 0:
+                            lhs = w4_sb[:, b, 2 * m * P : 2 * (m + 1) * P].bitcast(FP4X4)
+                            lhs_scale = w4_plane[:, b, cols]
+                            codes, scales = x_q[b, half]
+                        else:
+                            lhs = v2_codes[b][:, cols].bitcast(FP8X4)
+                            lhs_scale = v2_scales[4 * b :, cols]
+                            codes, scales = page_q[b, half]
+                        nc.tensor.matmul_mx(
+                            out=e_banks[m, half][:], lhsT=lhs, lhsT_scale=lhs_scale,
+                            rhs=codes[:].bitcast(FP8X4), rhs_scale=scales[:],
+                            start=(b == 0 and product == 0), stop=(b == R_PASSES - 1 and product == 1),
+                        )
+
+        scores = []
+        for m in range(M_TILES):
+            e = keep.tile([P, T2], F32, name=f"scores{m}", tag=f"page_slot0{m}", align_bytes=64)
+            for half in range(HALVES):
+                nc.scalar.copy(e[:, half * HALF : (half + 1) * HALF], e_banks[m, half][:])
+            scores.append(e)
+        for m in range(M_TILES):
+            seaward = ring.tile([P, S], F32, name="seaward")
+            landward = ring.tile([P, S], F32, name="landward")
+            nc.vector.tensor_copy(seaward[:], scores[m][:].indirect(p1[:]))
+            nc.vector.tensor_copy(landward[:], scores[m][:].indirect(p2[:]))
+            larger = ring.tile([P, S], F32, name="larger", tag="root")
+            nc.vector.tensor_tensor(larger[:], seaward[:], landward[:], ALU.max)
+            result = ring.tile([P, S], F32, name="result", tag="h", bufs=3)
+            nc.scalar.activation(result[:], larger[:], ACT.Identity, bias=neg_level[:, m : m + 1])
+            nc.sync.dma_start(out[m * P : (m + 1) * P, :], result[:])

@@ -1,6 +1,7 @@
 from contextlib import ExitStack
 
 import concourse.mybir as mybir
+from concourse.masks import make_identity
 
 K, H, T, S, T2, M = 1536, 1024, 2048, 512, 1024, 512
 FLOPS = 2 * K * H * S + 2 * 2 * H * M * T2
@@ -42,9 +43,9 @@ def tile_list_mangrove_stand_scores_kernel(
             nc.sync.dma_start(tile[:], src)
             return tile
 
-        def load_scale_rows(plane, src, passes):
+        def load_scale_rows(queue, plane, src, passes):
             for q in range(4):
-                nc.sync.dma_start(
+                queue.dma_start(
                     plane[32 * q : 32 * q + 4 * passes, :].bitcast(I32),
                     src[:, 4 * q : 4 * q + 4, :].bitcast(I32),
                 )
@@ -76,19 +77,25 @@ def tile_list_mangrove_stand_scores_kernel(
             nc.vector.tensor_copy(picked[:], window[:].indirect(offsets[:]))
             return picked
 
-        def quantise(name, grouped):
-            codes = keep.tile([P, HALF], U32, name=name + "_codes", align_bytes=64)
+        def quantise(name, grouped, tag=""):
+            codes = keep.tile([P, HALF], U32, name=name + "_codes", tag=tag, align_bytes=64)
             scales = keep.tile([P, HALF], U8, name=name + "_scales", align_bytes=64)
             nc.vector.quantize_mx(out=codes[:].bitcast(FP8X4), scales=scales[:], in_=grouped[:])
             return codes, scales
 
-        def group_w1(raw):
+        def group_w1(raw, copy):
             grouped = ring.tile([P, PACK * PASS], BF16, name="w1_grouped", align_bytes=64)
-            nc.scalar.copy(
+            copy(
                 grouped[:].rearrange("p (t m j) -> p m j t", t=PACK, j=PACK),
                 raw[:].rearrange("p j (m t) -> p m j t", t=PACK),
             )
             return grouped
+
+        def entries(part):
+            return slice(part * S // 2, (part + 1) * S // 2)
+
+        def list_part(offsets, part):
+            return offsets[:, part * S // 32 : (part + 1) * S // 32]
 
         def bank(i, name):
             return psum.tile([P, HALF], F32, name=name, tag=f"bank{i}")
@@ -99,37 +106,69 @@ def tile_list_mangrove_stand_scores_kernel(
         for plane in (v_plane, v2_plane, w4_plane):
             nc.vector.memset(plane[:].bitcast(I32), 0)
 
-        idx = load_list("idx", offs)
-        w1_raw, v_words, page, gm_sb = {}, {}, {}, {}
-        for a in range(K_PASSES):
-            w1_raw[0, a] = load_w1(0, a)
-            if a == 0:
-                load_scale_rows(v_plane, tab_scales, K_PASSES)
-            v_words[a] = load_table_words(tab_words, a, f"v_words{a}", f"tab_slot{a}")
+        ident = keep.tile([P, P], F32, name="ident")
+        make_identity(nc, ident[:])
+
+        wgs_rows = ring.tile([P, S], F32, name="wgs_rows", tag="root")
+        nc.sync.dma_start(wgs_rows[:], wgs)
         gain_sb = keep.tile([P, R_PASSES, PACK], F32, name="gain_sb")
         nc.sync.dma_start(gain_sb[:], gain.rearrange("(b p t) -> p b t", b=R_PASSES, t=PACK))
+        w1_raw, v_words, page, gm_sb = {}, {}, {}, {}
+        w1_raw[0, 0] = load_w1(0, 0)
+        idx = load_list("idx", offs)
+        w1_raw[0, 1] = load_w1(0, 1)
+        load_scale_rows(nc.sync, v_plane, tab_scales, K_PASSES)
+        v_words[0] = load_table_words(tab_words, 0, "v_words0", "tab_slot0")
+        w1_raw[0, 2] = load_w1(0, 2)
+        v_words[1] = load_table_words(tab_words, 1, "v_words1", "tab_slot1")
+        v_words[2] = load_table_words(tab_words, 2, "v_words2", "tab_slot2")
         idx3 = load_list("idx3", offs3)
-        wgs_sb = keep.tile([P, PACK, S], F32, name="wgs_sb", align_bytes=64)
-        for q in (0, 2, 1, 3):
-            nc.sync.dma_start(wgs_sb[32 * q : 32 * q + 32, :, :], wgs.rearrange("(q t) j -> q t j", t=PACK))
         page[0, 0] = load_page(0, 0)
-        page[0, 1] = load_page(0, 1)
 
-        v_scales = gather("v_scales", v_plane, idx, U8)
+        turned = psum.tile([P, S // P, P], F32, name="turned", tag="bank4")
+        for c in range(S // P):
+            nc.tensor.transpose(turned[:, c, :], wgs_rows[:, c * P : (c + 1) * P], ident[:])
+        repeated = keep.tile([P, S // P, 4, P], F32, name="repeated", tag="gm_slot0", align_bytes=64)
+        nc.scalar.copy(repeated[:], turned[:].unsqueeze(2).to_broadcast([P, S // P, 4, P]))
+        dealt = []
+        for t in range(PACK):
+            rows = bank(PACK + t, f"dealt{t}")
+            for c in range(S // P):
+                columns = repeated[:, c, :, :].rearrange("p q r -> p (q r)")[:, t::PACK]
+                nc.tensor.transpose(rows[:, c * P : (c + 1) * P], columns, ident[:])
+            dealt.append(rows)
+        weight = {}
+
+        def weigh(b, t):
+            weight[b, t] = keep.tile([P, S], F32, name=f"weight{b}{t}", tag=f"weight_slot{b}{t}", align_bytes=64)
+            nc.scalar.activation(weight[b, t][:], dealt[t][:], ACT.Copy, scale=gain_sb[:, b, t : t + 1])
+
         v_codes, w1_q = {}, {}
+        w1_q[0, 0] = quantise("w1_00", group_w1(w1_raw[0, 0], nc.vector.tensor_copy))
+        v_scales = gather("v_scales", v_plane, idx, U8)
         for a in range(K_PASSES):
-            w1_q[0, a] = quantise(f"w1_0{a}", group_w1(w1_raw[0, a]))
-            v_codes[a] = gather(f"v_codes{a}", v_words[a], idx, U32)
+            if a > 0:
+                w1_q[0, a] = quantise(f"w1_0{a}", group_w1(w1_raw[0, a], nc.vector.tensor_copy))
+            if a < K_PASSES - 1:
+                v_codes[a] = gather(f"v_codes{a}", v_words[a], idx, U32)
+        last = K_PASSES - 1
+        v_codes[last] = keep.tile([P, S], U32, name="v_codes_last", align_bytes=64)
+        for part in range(2):
+            nc.vector.tensor_copy(v_codes[last][:, entries(part)], v_words[last][:].indirect(list_part(idx, part)))
+        for b in range(R_PASSES):
+            for t in range(PACK):
+                weigh(b, t)
 
         w1_raw[1, 0] = load_w1(1, 0)
+        page[0, 1] = load_page(0, 1)
         w1_raw[1, 1] = load_w1(1, 1)
-        page[0, 2] = load_page(0, 2)
         w1_raw[1, 2] = load_w1(1, 2)
+        page[0, 2] = load_page(0, 2)
+        gm_sb[0, 0] = load_gm(0, 0, "gm_slot0")
         page[0, 3] = load_page(0, 3)
-        for half in range(HALVES):
-            gm_sb[0, half] = load_gm(0, half, f"gm_slot{half}")
-        for t in range(PACK):
-            page[1, t] = load_page(1, t)
+        gm_sb[0, 1] = load_gm(0, 1, "gm_slot1")
+        page[1, 0] = load_page(1, 0)
+        page[1, 1] = load_page(1, 1)
         for half in range(HALVES):
             gm_sb[1, half] = load_gm(1, half, f"tab_slot{half}")
         idx2 = load_list("idx2", offs2)
@@ -137,41 +176,43 @@ def tile_list_mangrove_stand_scores_kernel(
         p2 = load_list("p2", pos2)
         w4_sb = keep.tile([P, R_PASSES, 2 * M], U8, name="w4_sb", align_bytes=64)
         nc.sync.dma_start(w4_sb[:].bitcast(I32), w4_words.rearrange("a p c -> p a c").bitcast(I32))
-        load_scale_rows(v2_plane, tab2_scales, R_PASSES)
+        load_scale_rows(nc.sync, v2_plane, tab2_scales, R_PASSES)
         for q in range(4):
             nc.sync.dma_start(
                 w4_plane[32 * q : 32 * q + 4, :, :].bitcast(I32),
                 w4_scales[:, 4 * q : 4 * q + 4, :].rearrange("a r c -> r a c").bitcast(I32),
             )
 
-        def first_stage(b):
-            sums = []
-            for t in range(PACK):
-                d = bank(PACK * b + t, f"d{b}{t}")
-                cols = slice(t * P, (t + 1) * P)
-                for a in range(K_PASSES):
-                    codes, scales = w1_q[b, a]
-                    nc.tensor.matmul_mx(
-                        out=d[:],
-                        lhsT=codes[:, cols].bitcast(FP8X4), lhsT_scale=scales[:, cols],
-                        rhs=v_codes[a][:].bitcast(FP8X4), rhs_scale=v_scales[4 * a :, :],
-                        start=(a == 0), stop=(a == K_PASSES - 1),
-                    )
-                sums.append(d)
-            return sums
+        def first_stage(b, t, bank_index, js):
+            d = psum.tile([P, js.stop - js.start], F32, name=f"d{b}{t}_{js.start}", tag=f"bank{bank_index}")
+            cols = slice(t * P, (t + 1) * P)
+            for a in range(K_PASSES):
+                codes, scales = w1_q[b, a]
+                nc.tensor.matmul_mx(
+                    out=d[:],
+                    lhsT=codes[:, cols].bitcast(FP8X4), lhsT_scale=scales[:, cols],
+                    rhs=v_codes[a][:, js].bitcast(FP8X4), rhs_scale=v_scales[4 * a :, js],
+                    start=(a == 0), stop=(a == K_PASSES - 1),
+                )
+            return d
+
+        def root_tile(b, t):
+            return keep.tile([P, S], F32, name=f"root{b}{t}", tag=f"root_slot{t}", align_bytes=64)
+
+        def take_root(d, size, root):
+            nc.scalar.activation(size, d[:], ACT.Abs)
+            nc.scalar.activation(root, size, ACT.Sqrt)
 
         def features(d, b, t):
-            root = ring.tile([P, S], F32, name="root")
-            nc.scalar.activation(root[:], d[:], ACT.Abs)
-            nc.scalar.activation(root[:], root[:], ACT.Sqrt)
-            h = ring.tile([P, S], F32, name="h", bufs=3)
-            nc.scalar.activation(h[:], root[:], ACT.Copy, scale=gain_sb[:, b, t : t + 1])
-            return h
+            size = ring.tile([P, S], F32, name="size", tag="root")
+            root = root_tile(b, t)
+            take_root(d, size[:], root[:])
+            return root
 
         def scatter(h, b, t):
-            nc.vector.tensor_tensor(page[b, t][:].indirect(idx3[:]), h[:], wgs_sb[:, t, :], ALU.mult)
+            nc.vector.tensor_tensor(page[b, t][:].indirect(idx3[:]), h[:], weight[b, t][:], ALU.mult)
 
-        joined = [keep.tile([P, PACK, T2], F32, name=f"joined{b}", align_bytes=64) for b in range(R_PASSES)]
+        joined = {}
 
         def join(b, t):
             nc.scalar.copy(joined[b][:, t, :], page[b, t][:])
@@ -184,79 +225,108 @@ def tile_list_mangrove_stand_scores_kernel(
 
         page_q, x_q = {}, {}
 
-        def second_stage_operands(b):
-            grouped = {}
-            for half in range(HALVES):
-                rows = walk_rows(joined[b][:, :, half * HALF : (half + 1) * HALF])
-                x_grouped = ring.tile([P, PACK * HALF], BF16, name="x_grouped", align_bytes=64)
-                nc.vector.tensor_tensor(walk_words(x_grouped[:]), rows, walk_rows(gm_sb[b, half][:]), ALU.mult)
-                page_grouped = ring.tile([P, PACK * HALF], BF16, name="page_grouped", align_bytes=64)
-                nc.scalar.activation(walk_words(page_grouped[:]), rows, ACT.Copy)
-                grouped[half] = (x_grouped, page_grouped)
-            for half in range(HALVES):
-                x_q[b, half] = quantise(f"x{b}{half}", grouped[half][0])
-            for half in range(HALVES):
-                page_q[b, half] = quantise(f"page_q{b}{half}", grouped[half][1])
+        def group_x(b, half):
+            grouped = ring.tile([P, PACK * HALF], BF16, name="x_grouped", align_bytes=64)
+            rows = walk_rows(joined[b][:, :, half * HALF : (half + 1) * HALF])
+            nc.vector.tensor_tensor(walk_words(grouped[:]), rows, walk_rows(gm_sb[b, half][:]), ALU.mult)
+            return grouped
 
-        d0 = first_stage(0)
-        h = {(0, 0): features(d0[0], 0, 0), (0, 1): features(d0[1], 0, 1)}
-        scatter(h[0, 0], 0, 0)
-        h[0, 2] = features(d0[2], 0, 2)
-        join(0, 0)
+        def group_page(b, half):
+            grouped = ring.tile([P, PACK * HALF], BF16, name="page_grouped", align_bytes=64)
+            rows = walk_rows(joined[b][:, :, half * HALF : (half + 1) * HALF])
+            nc.scalar.activation(walk_words(grouped[:]), rows, ACT.Copy)
+            return grouped
+
+        def gather_candidates(part, pool, words_tag, scales_tag):
+            picks = list_part(idx2, part)
+            words = pool.tile([P, R_PASSES, M // 2], U32, name=f"v2_codes{part}", tag=words_tag, align_bytes=64)
+            scales = pool.tile([P, M // 2], U8, name=f"v2_scales{part}", tag=scales_tag, align_bytes=64)
+            for b in range(R_PASSES):
+                nc.vector.tensor_copy(words[:, b, :], v2_words[b][:].indirect(picks))
+            nc.vector.tensor_copy(scales[:], v2_plane[:].indirect(picks))
+            return words, scales
+
+        whole = slice(0, S)
+        first = [first_stage(0, 0, PACK * part, entries(part)) for part in range(2)]
+        d0 = {t: first_stage(0, t, t, whole) for t in range(1, PACK)}
+        h = {(0, 0): root_tile(0, 0)}
+        size = keep.tile([P, S // 2], F32, name="size_first")
+        for part in range(2):
+            take_root(first[part], size[:], h[0, 0][:, entries(part)])
+        for t in range(1, PACK):
+            h[0, t] = features(d0[t], 0, t)
+        for part in range(2):
+            nc.vector.tensor_tensor(
+                page[0, 0][:].indirect(list_part(idx3, part)),
+                h[0, 0][:, entries(part)], weight[0, 0][:, entries(part)], ALU.mult,
+            )
         scatter(h[0, 1], 0, 1)
-        h[0, 3] = features(d0[3], 0, 3)
-        w1_q[1, 0] = quantise("w1_10", group_w1(w1_raw[1, 0]))
-        join(0, 1)
+        w1_q[1, 0] = quantise("w1_10", group_w1(w1_raw[1, 0], nc.scalar.copy))
+        w1_grouped = [group_w1(w1_raw[1, a], nc.scalar.copy) for a in (1, 2)]
         scatter(h[0, 2], 0, 2)
-        w1_q[1, 1] = quantise("w1_11", group_w1(w1_raw[1, 1]))
-        w1_q[1, 2] = quantise("w1_12", group_w1(w1_raw[1, 2]))
-        join(0, 2)
         scatter(h[0, 3], 0, 3)
-        join(0, 3)
+        w1_q[1, 1] = quantise("w1_11", w1_grouped[0], "weight_slot03")
+        w1_q[1, 2] = quantise("w1_12", w1_grouped[1], "root_slot3")
+        joined[0] = keep.tile([P, PACK, T2], F32, name="joined0", tag="w1_slot2", align_bytes=64)
+        joined[1] = keep.tile([P, PACK, T2], F32, name="joined1", align_bytes=64)
+        for t in range(PACK):
+            join(0, t)
         v2_words = [load_table_words(tab2_words, b, f"v2_words{b}", f"w1_slot{b}") for b in range(R_PASSES)]
+        page[1, 2] = load_page(1, 2)
+        page[1, 3] = load_page(1, 3)
         level_sb = keep.tile([P, M_TILES], F32, name="level_sb")
         with nc.allow_non_contiguous_dma(reason="one level for each partition and tile of rows"):
             nc.sync.dma_start(level_sb[:], level.rearrange("(m p) -> p m", p=P))
-        d1 = first_stage(1)
+        d1 = [first_stage(1, t, PACK + t, whole) for t in range(PACK)]
         h[1, 0] = features(d1[0], 1, 0)
         h[1, 1] = features(d1[1], 1, 1)
-        second_stage_operands(0)
-        scatter(h[1, 0], 1, 0)
+        x_grouped = [group_x(0, half) for half in range(HALVES)]
+        page_grouped = [group_page(0, half) for half in range(HALVES)]
+        for half in range(HALVES):
+            x_q[0, half] = quantise(f"x0{half}", x_grouped[half])
         h[1, 2] = features(d1[2], 1, 2)
-        join(1, 0)
-        scatter(h[1, 1], 1, 1)
         h[1, 3] = features(d1[3], 1, 3)
-        join(1, 1)
-        scatter(h[1, 2], 1, 2)
-        join(1, 2)
-        scatter(h[1, 3], 1, 3)
-        join(1, 3)
-        v2_scales = gather("v2_scales", v2_plane, idx2, U8)
-        v2_codes = [gather(f"v2_codes{b}", v2_words[b], idx2, U32) for b in range(R_PASSES)]
-        second_stage_operands(1)
+        for t in range(PACK):
+            scatter(h[1, t], 1, t)
+            if t < HALVES:
+                page_q[0, t] = quantise(f"page_q0{t}", page_grouped[t])
+            join(1, t)
+        candidates = [gather_candidates(0, keep, "weight_slot13", "root_slot3")]
+        x_grouped = [group_x(1, half) for half in range(HALVES)]
+        page_grouped = [group_page(1, half) for half in range(HALVES)]
+        for half in range(HALVES):
+            page_q[1, half] = quantise(f"page_q1{half}", page_grouped[half])
+            x_q[1, half] = quantise(f"x1{half}", x_grouped[half])
+        candidates.append(gather_candidates(1, ring, "x_grouped", "x_grouped"))
 
         neg_level = keep.tile([P, M_TILES], F32, name="neg_level")
         nc.scalar.activation(neg_level[:], level_sb[:], ACT.Copy, scale=-1.0)
 
         e_banks = {(m, half): bank(HALVES * m + half, f"e{m}{half}") for m in range(M_TILES) for half in range(HALVES)}
-        for b in range(R_PASSES):
-            for product in range(2):
-                for m in range(M_TILES):
-                    cols = slice(m * P, (m + 1) * P)
-                    for half in range(HALVES):
-                        if product == 0:
-                            lhs = w4_sb[:, b, 2 * m * P : 2 * (m + 1) * P].bitcast(FP4X4)
-                            lhs_scale = w4_plane[:, b, cols]
-                            codes, scales = x_q[b, half]
-                        else:
-                            lhs = v2_codes[b][:, cols].bitcast(FP8X4)
-                            lhs_scale = v2_scales[4 * b :, cols]
-                            codes, scales = page_q[b, half]
-                        nc.tensor.matmul_mx(
-                            out=e_banks[m, half][:], lhsT=lhs, lhsT_scale=lhs_scale,
-                            rhs=codes[:].bitcast(FP8X4), rhs_scale=scales[:],
-                            start=(b == 0 and product == 0), stop=(b == R_PASSES - 1 and product == 1),
-                        )
+
+        def second_stage(m, steps):
+            for step, (product, b) in steps:
+                for half in range(HALVES):
+                    if product == "x":
+                        lhs = w4_sb[:, b, 2 * m * P : 2 * (m + 1) * P].bitcast(FP4X4)
+                        lhs_scale = w4_plane[:, b, m * P : (m + 1) * P]
+                        codes, scales = x_q[b, half]
+                    else:
+                        words, planes = candidates[m // 2]
+                        cols = slice(m % 2 * P, (m % 2 + 1) * P)
+                        lhs = words[:, b, cols].bitcast(FP8X4)
+                        lhs_scale = planes[4 * b :, cols]
+                        codes, scales = page_q[b, half]
+                    nc.tensor.matmul_mx(
+                        out=e_banks[m, half][:], lhsT=lhs, lhsT_scale=lhs_scale,
+                        rhs=codes[:].bitcast(FP8X4), rhs_scale=scales[:],
+                        start=(step == 0), stop=(step == 2 * R_PASSES - 1),
+                    )
+
+        early = list(enumerate([("x", 0), ("page", 0), ("page", 1), ("x", 1)]))
+        late = list(enumerate([("x", 0), ("x", 1), ("page", 0), ("page", 1)]))
+        for m in range(M_TILES):
+            second_stage(m, early if m < 2 else late)
 
         scores = []
         for m in range(M_TILES):
@@ -264,13 +334,18 @@ def tile_list_mangrove_stand_scores_kernel(
             for half in range(HALVES):
                 nc.scalar.copy(e[:, half * HALF : (half + 1) * HALF], e_banks[m, half][:])
             scores.append(e)
-        for m in range(M_TILES):
-            seaward = ring.tile([P, S], F32, name="seaward")
-            landward = ring.tile([P, S], F32, name="landward")
-            nc.vector.tensor_copy(seaward[:], scores[m][:].indirect(p1[:]))
-            nc.vector.tensor_copy(landward[:], scores[m][:].indirect(p2[:]))
-            larger = ring.tile([P, S], F32, name="larger", tag="root")
-            nc.vector.tensor_tensor(larger[:], seaward[:], landward[:], ALU.max)
-            result = ring.tile([P, S], F32, name="result", tag="h", bufs=3)
-            nc.scalar.activation(result[:], larger[:], ACT.Identity, bias=neg_level[:, m : m + 1])
+        for m, e in enumerate(scores):
+            seaward = keep.tile([P, S], F32, name=f"seaward{m}", tag=f"weight_slot0{m}", align_bytes=64)
+            landward = keep.tile([P, S], F32, name=f"landward{m}", tag=f"root_slot{m}" if m < 3 else "weight_slot10", align_bytes=64)
+            nc.vector.tensor_copy(seaward[:], e[:].indirect(p1[:]))
+            nc.vector.tensor_copy(landward[:], e[:].indirect(p2[:]))
+            if m < 2:
+                above = keep.tile([P, S], F32, name=f"above{m}", tag=f"page_q1{1 - m}_codes", align_bytes=64)
+            else:
+                above = ring.tile([P, S], F32, name=f"above{m}", tag="x_grouped", align_bytes=64)
+            nc.scalar.activation(above[:], seaward[:], ACT.Identity, bias=neg_level[:, m : m + 1])
+            result = keep.tile([P, S], F32, name=f"result{m}", tag=f"x{m // 2}{m % 2}_codes", align_bytes=64)
+            nc.vector.scalar_tensor_tensor(
+                result[:], landward[:], level_sb[:, m : m + 1], above[:], ALU.subtract, ALU.max
+            )
             nc.sync.dma_start(out[m * P : (m + 1) * P, :], result[:])

@@ -77,11 +77,14 @@ def tile_list_mangrove_stand_scores_kernel(
             nc.vector.tensor_copy(picked[:], window[:].indirect(offsets[:]))
             return picked
 
+        def quantise_into(name, codes, grouped):
+            scales = keep.tile([P, HALF], U8, name=name + "_scales", align_bytes=64)
+            nc.vector.quantize_mx(out=codes.bitcast(FP8X4), scales=scales[:], in_=grouped[:])
+            return codes, scales
+
         def quantise(name, grouped, tag=""):
             codes = keep.tile([P, HALF], U32, name=name + "_codes", tag=tag, align_bytes=64)
-            scales = keep.tile([P, HALF], U8, name=name + "_scales", align_bytes=64)
-            nc.vector.quantize_mx(out=codes[:].bitcast(FP8X4), scales=scales[:], in_=grouped[:])
-            return codes, scales
+            return quantise_into(name, codes[:], grouped)
 
         def group_w1(raw, copy):
             grouped = ring.tile([P, PACK * PASS], BF16, name="w1_grouped", align_bytes=64)
@@ -167,21 +170,10 @@ def tile_list_mangrove_stand_scores_kernel(
         gm_sb[0, 0] = load_gm(0, 0, "gm_slot0")
         page[0, 3] = load_page(0, 3)
         gm_sb[0, 1] = load_gm(0, 1, "gm_slot1")
-        page[1, 0] = load_page(1, 0)
-        page[1, 1] = load_page(1, 1)
-        for half in range(HALVES):
-            gm_sb[1, half] = load_gm(1, half, f"tab_slot{half}")
+        for t in range(PACK - 1):
+            page[1, t] = load_page(1, t)
         idx2 = load_list("idx2", offs2)
-        p1 = load_list("p1", pos1)
-        p2 = load_list("p2", pos2)
-        w4_sb = keep.tile([P, R_PASSES, 2 * M], U8, name="w4_sb", align_bytes=64)
-        nc.sync.dma_start(w4_sb[:].bitcast(I32), w4_words.rearrange("a p c -> p a c").bitcast(I32))
         load_scale_rows(nc.sync, v2_plane, tab2_scales, R_PASSES)
-        for q in range(4):
-            nc.sync.dma_start(
-                w4_plane[32 * q : 32 * q + 4, :, :].bitcast(I32),
-                w4_scales[:, 4 * q : 4 * q + 4, :].rearrange("a r c -> r a c").bitcast(I32),
-            )
 
         def first_stage(b, t, bank_index, js):
             d = psum.tile([P, js.stop - js.start], F32, name=f"d{b}{t}_{js.start}", tag=f"bank{bank_index}")
@@ -212,6 +204,14 @@ def tile_list_mangrove_stand_scores_kernel(
         def scatter(h, b, t):
             nc.vector.tensor_tensor(page[b, t][:].indirect(idx3[:]), h[:], weight[b, t][:], ALU.mult)
 
+        def weighted(engine, h, b, t, tag):
+            values = keep.tile([P, S], F32, name=f"values{b}{t}", tag=tag, align_bytes=64)
+            engine.tensor_tensor(values[:], h[:], weight[b, t][:], ALU.mult)
+            return values
+
+        def scatter_values(values, b, t):
+            nc.vector.tensor_copy(page[b, t][:].indirect(idx3[:]), values[:])
+
         joined = {}
 
         def join(b, t):
@@ -227,8 +227,16 @@ def tile_list_mangrove_stand_scores_kernel(
 
         def group_x(b, half):
             grouped = ring.tile([P, PACK * HALF], BF16, name="x_grouped", align_bytes=64)
-            rows = walk_rows(joined[b][:, :, half * HALF : (half + 1) * HALF])
-            nc.vector.tensor_tensor(walk_words(grouped[:]), rows, walk_rows(gm_sb[b, half][:]), ALU.mult)
+            if b == 0:
+                for part in range(2):
+                    n0 = part * HALF // 2
+                    rows = walk_rows(joined[b][:, :, half * HALF + n0 : half * HALF + n0 + HALF // 2])
+                    factors = walk_rows(gm_sb[b, half][:, :, n0 : n0 + HALF // 2])
+                    words = walk_words(grouped[:, PACK * n0 : PACK * (n0 + HALF // 2)])
+                    nc.gpsimd.tensor_tensor(words, rows, factors, ALU.mult)
+            else:
+                rows = walk_rows(joined[b][:, :, half * HALF : (half + 1) * HALF])
+                nc.vector.tensor_tensor(walk_words(grouped[:]), rows, walk_rows(gm_sb[b, half][:]), ALU.mult)
             return grouped
 
         def group_page(b, half):
@@ -264,34 +272,45 @@ def tile_list_mangrove_stand_scores_kernel(
         w1_q[1, 0] = quantise("w1_10", group_w1(w1_raw[1, 0], nc.scalar.copy))
         w1_grouped = [group_w1(w1_raw[1, a], nc.scalar.copy) for a in (1, 2)]
         scatter(h[0, 2], 0, 2)
+        w1_q[1, 1] = quantise("w1_11", w1_grouped[0], "weight_slot02")
+        w1_q[1, 2] = quantise("w1_12", w1_grouped[1])
         scatter(h[0, 3], 0, 3)
-        w1_q[1, 1] = quantise("w1_11", w1_grouped[0], "weight_slot03")
-        w1_q[1, 2] = quantise("w1_12", w1_grouped[1], "root_slot3")
         joined[0] = keep.tile([P, PACK, T2], F32, name="joined0", tag="w1_slot2", align_bytes=64)
         joined[1] = keep.tile([P, PACK, T2], F32, name="joined1", align_bytes=64)
-        for t in range(PACK):
-            join(0, t)
         v2_words = [load_table_words(tab2_words, b, f"v2_words{b}", f"w1_slot{b}") for b in range(R_PASSES)]
-        page[1, 2] = load_page(1, 2)
+        for half in range(HALVES):
+            gm_sb[1, half] = load_gm(1, half, f"tab_slot{half}")
         page[1, 3] = load_page(1, 3)
+        w4_sb = keep.tile([P, R_PASSES, 2 * M], U8, name="w4_sb", align_bytes=64)
+        nc.sync.dma_start(w4_sb[:].bitcast(I32), w4_words.rearrange("a p c -> p a c").bitcast(I32))
+        for q in range(4):
+            nc.sync.dma_start(
+                w4_plane[32 * q : 32 * q + 4, :, :].bitcast(I32),
+                w4_scales[:, 4 * q : 4 * q + 4, :].rearrange("a r c -> r a c").bitcast(I32),
+            )
+        p1 = load_list("p1", pos1)
+        p2 = load_list("p2", pos2)
         level_sb = keep.tile([P, M_TILES], F32, name="level_sb")
         with nc.allow_non_contiguous_dma(reason="one level for each partition and tile of rows"):
             nc.sync.dma_start(level_sb[:], level.rearrange("(m p) -> p m", p=P))
         d1 = [first_stage(1, t, PACK + t, whole) for t in range(PACK)]
-        h[1, 0] = features(d1[0], 1, 0)
-        h[1, 1] = features(d1[1], 1, 1)
+        values = []
+        for t in range(PACK):
+            engine = nc.vector if t == 0 else nc.gpsimd
+            values.append(weighted(engine, features(d1[t], 1, t), 1, t, f"values_slot{t}" if t else "weight_slot03"))
+        for t in range(PACK):
+            join(0, t)
         x_grouped = [group_x(0, half) for half in range(HALVES)]
         page_grouped = [group_page(0, half) for half in range(HALVES)]
-        for half in range(HALVES):
-            x_q[0, half] = quantise(f"x0{half}", x_grouped[half])
-        h[1, 2] = features(d1[2], 1, 2)
-        h[1, 3] = features(d1[3], 1, 3)
         for t in range(PACK):
-            scatter(h[1, t], 1, t)
-            if t < HALVES:
-                page_q[0, t] = quantise(f"page_q0{t}", page_grouped[t])
+            scatter_values(values[t], 1, t)
             join(1, t)
-        candidates = [gather_candidates(0, keep, "weight_slot13", "root_slot3")]
+        candidates = [gather_candidates(0, keep, "values_slot2", "values_slot1")]
+        codes = keep.tile([P, 2 * HALVES, HALF], U32, name="second_codes0", tag="values_slot3", align_bytes=64)
+        for half in range(HALVES):
+            page_q[0, half] = quantise_into(f"page_q0{half}", codes[:, half, :], page_grouped[half])
+        for half in range(HALVES):
+            x_q[0, half] = quantise_into(f"x0{half}", codes[:, HALVES + half, :], x_grouped[half])
         x_grouped = [group_x(1, half) for half in range(HALVES)]
         page_grouped = [group_page(1, half) for half in range(HALVES)]
         for half in range(HALVES):
@@ -319,7 +338,7 @@ def tile_list_mangrove_stand_scores_kernel(
                         codes, scales = page_q[b, half]
                     nc.tensor.matmul_mx(
                         out=e_banks[m, half][:], lhsT=lhs, lhsT_scale=lhs_scale,
-                        rhs=codes[:].bitcast(FP8X4), rhs_scale=scales[:],
+                        rhs=codes.bitcast(FP8X4), rhs_scale=scales[:],
                         start=(step == 0), stop=(step == 2 * R_PASSES - 1),
                     )
 
@@ -336,7 +355,7 @@ def tile_list_mangrove_stand_scores_kernel(
             scores.append(e)
         for m, e in enumerate(scores):
             seaward = keep.tile([P, S], F32, name=f"seaward{m}", tag=f"weight_slot0{m}", align_bytes=64)
-            landward = keep.tile([P, S], F32, name=f"landward{m}", tag=f"root_slot{m}" if m < 3 else "weight_slot10", align_bytes=64)
+            landward = keep.tile([P, S], F32, name=f"landward{m}", tag=f"root_slot{m}", align_bytes=64)
             nc.vector.tensor_copy(seaward[:], e[:].indirect(p1[:]))
             nc.vector.tensor_copy(landward[:], e[:].indirect(p2[:]))
             if m < 2:
@@ -344,7 +363,7 @@ def tile_list_mangrove_stand_scores_kernel(
             else:
                 above = ring.tile([P, S], F32, name=f"above{m}", tag="x_grouped", align_bytes=64)
             nc.scalar.activation(above[:], seaward[:], ACT.Identity, bias=neg_level[:, m : m + 1])
-            result = keep.tile([P, S], F32, name=f"result{m}", tag=f"x{m // 2}{m % 2}_codes", align_bytes=64)
+            result = keep.tile([P, S], F32, name=f"result{m}", tag=f"weight_slot1{m}", align_bytes=64)
             nc.vector.scalar_tensor_tensor(
                 result[:], landward[:], level_sb[:, m : m + 1], above[:], ALU.subtract, ALU.max
             )

@@ -111,6 +111,8 @@ def tile_list_mangrove_stand_scores_kernel(
 
         ident = keep.tile([P, P], F32, name="ident")
         make_identity(nc, ident[:])
+        unread = keep.tile([P, 1], F32, name="unread")
+        nc.scalar.activation(unread[:], ident[:, 0:1], ACT.Sqrt)
 
         wgs_rows = ring.tile([P, S], F32, name="wgs_rows", tag="root")
         nc.sync.dma_start(wgs_rows[:], wgs)

from contextlib import ExitStack

import concourse.mybir as mybir
from concourse.masks import make_identity

K, H, T, S, T2, M = 1536, 1024, 2048, 512, 1024, 512
FLOPS = 2 * K * H * S + 2 * 2 * H * M * T2

F32 = mybir.dt.float32
BF16 = mybir.dt.bfloat16
I32 = mybir.dt.int32
U32 = mybir.dt.uint32
U16 = mybir.dt.uint16
U8 = mybir.dt.uint8
FP8X4 = mybir.dt.float8_e4m3fn_x4
FP4X4 = mybir.dt.float4_e2m1fn_x4
ACT = mybir.ActivationFunctionType
ALU = mybir.AluOpType

P = 128
PACK = 4
PASS = P * PACK
K_PASSES = K // PASS
R_PASSES = H // PASS
HALF = 512
HALVES = T2 // HALF
M_TILES = M // P


def tile_list_mangrove_stand_scores_kernel(
    tc, tab_words, tab_scales, offs, w1, gain, page0, wgs, offs3, tab2_words, tab2_scales, offs2,
    gm, w4_words, w4_scales, pos1, pos2, level, out,
):
    nc = tc.nc
    with ExitStack() as ctx:
        lists = ctx.enter_context(tc.tile_pool(name="lists", bufs=1))
        keep = ctx.enter_context(tc.tile_pool(name="keep", bufs=1))
        ring = ctx.enter_context(tc.tile_pool(name="ring", bufs=2))
        psum = ctx.enter_context(tc.psum_pool(name="psum", bufs=1))

        def load_list(name, src):
            tile = lists.tile([P, S // 16], U16, name=name)
            nc.sync.dma_start(tile[:], src)
            return tile

        def load_scale_rows(queue, plane, src, passes):
            for q in range(4):
                queue.dma_start(
                    plane[32 * q : 32 * q + 4 * passes, :].bitcast(I32),
                    src[:, 4 * q : 4 * q + 4, :].bitcast(I32),
                )

        def load_table_words(src, a, name, tag):
            words = keep.tile([P, T], U32, name=name, tag=tag, align_bytes=64)
            nc.sync.dma_start(words[:].bitcast(I32), src[a].rearrange("p n i -> p (n i)").bitcast(I32))
            return words

        def load_w1(b, a):
            raw = keep.tile([P, PACK, PASS], F32, name=f"w1_raw{b}{a}", tag=f"w1_slot{a}", align_bytes=64)
            src = w1[a * PASS : (a + 1) * PASS, b * PASS : (b + 1) * PASS]
            nc.sync.dma_start(raw[:], src.rearrange("(p j) c -> p j c", j=PACK))
            return raw

        def load_page(b, t):
            tile = keep.tile([P, T2], F32, name=f"page{b}{t}", tag=f"page_slot{b}{t}", align_bytes=64)
            nc.sync.dma_start(tile[:], page0.rearrange("(b p t) n -> b t p n", b=R_PASSES, t=PACK)[b, t])
            return tile

        def load_gm(b, half, tag):
            tile = keep.tile([P, PACK, HALF], F32, name=f"gm{b}{half}", tag=tag, align_bytes=64)
            src = gm[b * PASS : (b + 1) * PASS, half * HALF : (half + 1) * HALF]
            nc.sync.dma_start(tile[:], src.rearrange("(p t) n -> p t n", t=PACK))
            return tile

        def gather(name, window, offsets, dtype):
            picked = keep.tile([P, S], dtype, name=name, align_bytes=64)
            nc.vector.tensor_copy(picked[:], window[:].indirect(offsets[:]))
            return picked

        def quantise_into(name, codes, grouped):
            scales = keep.tile([P, HALF], U8, name=name + "_scales", align_bytes=64)
            nc.vector.quantize_mx(out=codes.bitcast(FP8X4), scales=scales[:], in_=grouped[:])
            return codes, scales

        def quantise(name, grouped, tag=""):
            codes = keep.tile([P, HALF], U32, name=name + "_codes", tag=tag, align_bytes=64)
            return quantise_into(name, codes[:], grouped)

        def group_w1(raw, copy):
            grouped = ring.tile([P, PACK * PASS], BF16, name="w1_grouped", align_bytes=64)
            copy(
                grouped[:].rearrange("p (t m j) -> p m j t", t=PACK, j=PACK),
                raw[:].rearrange("p j (m t) -> p m j t", t=PACK),
            )
            return grouped

        def entries(part):
            return slice(part * S // 2, (part + 1) * S // 2)

        def list_part(offsets, part):
            return offsets[:, part * S // 32 : (part + 1) * S // 32]

        def bank(i, name):
            return psum.tile([P, HALF], F32, name=name, tag=f"bank{i}")

        v_plane = keep.tile([P, T], U8, name="v_plane", align_bytes=64)
        v2_plane = keep.tile([P, T], U8, name="v2_plane", align_bytes=64)
        w4_plane = keep.tile([P, R_PASSES, M], U8, name="w4_plane", align_bytes=64)
        for plane in (v_plane, v2_plane, w4_plane):
            nc.vector.memset(plane[:].bitcast(I32), 0)

        ident = keep.tile([P, P], F32, name="ident")
        make_identity(nc, ident[:])
        unread = keep.tile([P, 1], F32, name="unread")
        nc.scalar.activation(unread[:], ident[:, 0:1], ACT.Sqrt)

        wgs_rows = ring.tile([P, S], F32, name="wgs_rows", tag="root")
        nc.sync.dma_start(wgs_rows[:], wgs)
        gain_sb = keep.tile([P, R_PASSES, PACK], F32, name="gain_sb")
        nc.sync.dma_start(gain_sb[:], gain.rearrange("(b p t) -> p b t", b=R_PASSES, t=PACK))
        w1_raw, v_words, page, gm_sb = {}, {}, {}, {}
        w1_raw[0, 0] = load_w1(0, 0)
        idx = load_list("idx", offs)
        w1_raw[0, 1] = load_w1(0, 1)
        load_scale_rows(nc.sync, v_plane, tab_scales, K_PASSES)
        v_words[0] = load_table_words(tab_words, 0, "v_words0", "tab_slot0")
        w1_raw[0, 2] = load_w1(0, 2)
        v_words[1] = load_table_words(tab_words, 1, "v_words1", "tab_slot1")
        v_words[2] = load_table_words(tab_words, 2, "v_words2", "tab_slot2")
        idx3 = load_list("idx3", offs3)
        page[0, 0] = load_page(0, 0)

        turned = psum.tile([P, S // P, P], F32, name="turned", tag="bank4")
        for c in range(S // P):
            nc.tensor.transpose(turned[:, c, :], wgs_rows[:, c * P : (c + 1) * P], ident[:])
        repeated = keep.tile([P, S // P, 4, P], F32, name="repeated", tag="gm_slot0", align_bytes=64)
        nc.scalar.copy(repeated[:], turned[:].unsqueeze(2).to_broadcast([P, S // P, 4, P]))
        dealt = []
        for t in range(PACK):
            rows = bank(PACK + t, f"dealt{t}")
            for c in range(S // P):
                columns = repeated[:, c, :, :].rearrange("p q r -> p (q r)")[:, t::PACK]
                nc.tensor.transpose(rows[:, c * P : (c + 1) * P], columns, ident[:])
            dealt.append(rows)
        weight = {}

        def weigh(b, t):
            weight[b, t] = keep.tile([P, S], F32, name=f"weight{b}{t}", tag=f"weight_slot{b}{t}", align_bytes=64)
            nc.scalar.activation(weight[b, t][:], dealt[t][:], ACT.Copy, scale=gain_sb[:, b, t : t + 1])

        v_codes, w1_q = {}, {}
        w1_q[0, 0] = quantise("w1_00", group_w1(w1_raw[0, 0], nc.vector.tensor_copy))
        v_scales = gather("v_scales", v_plane, idx, U8)
        for a in range(K_PASSES):
            if a > 0:
                w1_q[0, a] = quantise(f"w1_0{a}", group_w1(w1_raw[0, a], nc.vector.tensor_copy))
            if a < K_PASSES - 1:
                v_codes[a] = gather(f"v_codes{a}", v_words[a], idx, U32)
        last = K_PASSES - 1
        v_codes[last] = keep.tile([P, S], U32, name="v_codes_last", align_bytes=64)
        for part in range(2):
            nc.vector.tensor_copy(v_codes[last][:, entries(part)], v_words[last][:].indirect(list_part(idx, part)))
        for b in range(R_PASSES):
            for t in range(PACK):
                weigh(b, t)

        w1_raw[1, 0] = load_w1(1, 0)
        page[0, 1] = load_page(0, 1)
        w1_raw[1, 1] = load_w1(1, 1)
        w1_raw[1, 2] = load_w1(1, 2)
        page[0, 2] = load_page(0, 2)
        gm_sb[0, 0] = load_gm(0, 0, "gm_slot0")
        page[0, 3] = load_page(0, 3)
        gm_sb[0, 1] = load_gm(0, 1, "gm_slot1")
        for t in range(PACK - 1):
            page[1, t] = load_page(1, t)
        idx2 = load_list("idx2", offs2)
        load_scale_rows(nc.sync, v2_plane, tab2_scales, R_PASSES)

        def first_stage(b, t, bank_index, js):
            d = psum.tile([P, js.stop - js.start], F32, name=f"d{b}{t}_{js.start}", tag=f"bank{bank_index}")
            cols = slice(t * P, (t + 1) * P)
            for a in range(K_PASSES):
                codes, scales = w1_q[b, a]
                nc.tensor.matmul_mx(
                    out=d[:],
                    lhsT=codes[:, cols].bitcast(FP8X4), lhsT_scale=scales[:, cols],
                    rhs=v_codes[a][:, js].bitcast(FP8X4), rhs_scale=v_scales[4 * a :, js],
                    start=(a == 0), stop=(a == K_PASSES - 1),
                )
            return d

        def root_tile(b, t):
            return keep.tile([P, S], F32, name=f"root{b}{t}", tag=f"root_slot{t}", align_bytes=64)

        def take_root(d, size, root):
            nc.scalar.activation(size, d[:], ACT.Abs)
            nc.scalar.activation(root, size, ACT.Sqrt)

        def features(d, b, t):
            size = ring.tile([P, S], F32, name="size", tag="root")
            root = root_tile(b, t)
            take_root(d, size[:], root[:])
            return root

        def scatter(h, b, t):
            nc.vector.tensor_tensor(page[b, t][:].indirect(idx3[:]), h[:], weight[b, t][:], ALU.mult)

        def weighted(engine, h, b, t, tag):
            values = keep.tile([P, S], F32, name=f"values{b}{t}", tag=tag, align_bytes=64)
            engine.tensor_tensor(values[:], h[:], weight[b, t][:], ALU.mult)
            return values

        def scatter_values(values, b, t):
            nc.vector.tensor_copy(page[b, t][:].indirect(idx3[:]), values[:])

        joined = {}

        def join(b, t):
            nc.scalar.copy(joined[b][:, t, :], page[b, t][:])

        def walk_rows(ap):
            return ap.rearrange("p t (c i) -> p c t i", i=4)

        def walk_words(ap):
            return ap.rearrange("p (c i t) -> p c t i", i=4, t=PACK)

        page_q, x_q = {}, {}

        def group_x(b, half):
            grouped = ring.tile([P, PACK * HALF], BF16, name="x_grouped", align_bytes=64)
            if b == 0:
                for part in range(2):
                    n0 = part * HALF // 2
                    rows = walk_rows(joined[b][:, :, half * HALF + n0 : half * HALF + n0 + HALF // 2])
                    factors = walk_rows(gm_sb[b, half][:, :, n0 : n0 + HALF // 2])
                    words = walk_words(grouped[:, PACK * n0 : PACK * (n0 + HALF // 2)])
                    nc.gpsimd.tensor_tensor(words, rows, factors, ALU.mult)
            else:
                rows = walk_rows(joined[b][:, :, half * HALF : (half + 1) * HALF])
                nc.vector.tensor_tensor(walk_words(grouped[:]), rows, walk_rows(gm_sb[b, half][:]), ALU.mult)
            return grouped

        def group_page(b, half):
            grouped = ring.tile([P, PACK * HALF], BF16, name="page_grouped", align_bytes=64)
            rows = walk_rows(joined[b][:, :, half * HALF : (half + 1) * HALF])
            nc.scalar.activation(walk_words(grouped[:]), rows, ACT.Copy)
            return grouped

        def gather_candidates(part, pool, words_tag, scales_tag):
            picks = list_part(idx2, part)
            words = pool.tile([P, R_PASSES, M // 2], U32, name=f"v2_codes{part}", tag=words_tag, align_bytes=64)
            scales = pool.tile([P, M // 2], U8, name=f"v2_scales{part}", tag=scales_tag, align_bytes=64)
            for b in range(R_PASSES):
                nc.vector.tensor_copy(words[:, b, :], v2_words[b][:].indirect(picks))
            nc.vector.tensor_copy(scales[:], v2_plane[:].indirect(picks))
            return words, scales

        whole = slice(0, S)
        first = [first_stage(0, 0, PACK * part, entries(part)) for part in range(2)]
        d0 = {t: first_stage(0, t, t, whole) for t in range(1, PACK)}
        h = {(0, 0): root_tile(0, 0)}
        size = keep.tile([P, S // 2], F32, name="size_first")
        for part in range(2):
            take_root(first[part], size[:], h[0, 0][:, entries(part)])
        for t in range(1, PACK):
            h[0, t] = features(d0[t], 0, t)
        for part in range(2):
            nc.vector.tensor_tensor(
                page[0, 0][:].indirect(list_part(idx3, part)),
                h[0, 0][:, entries(part)], weight[0, 0][:, entries(part)], ALU.mult,
            )
        scatter(h[0, 1], 0, 1)
        w1_q[1, 0] = quantise("w1_10", group_w1(w1_raw[1, 0], nc.scalar.copy))
        w1_grouped = [group_w1(w1_raw[1, a], nc.scalar.copy) for a in (1, 2)]
        scatter(h[0, 2], 0, 2)
        w1_q[1, 1] = quantise("w1_11", w1_grouped[0], "weight_slot02")
        w1_q[1, 2] = quantise("w1_12", w1_grouped[1])
        scatter(h[0, 3], 0, 3)
        joined[0] = keep.tile([P, PACK, T2], F32, name="joined0", tag="w1_slot2", align_bytes=64)
        joined[1] = keep.tile([P, PACK, T2], F32, name="joined1", align_bytes=64)
        v2_words = [load_table_words(tab2_words, b, f"v2_words{b}", f"w1_slot{b}") for b in range(R_PASSES)]
        for half in range(HALVES):
            gm_sb[1, half] = load_gm(1, half, f"tab_slot{half}")
        page[1, 3] = load_page(1, 3)
        w4_sb = keep.tile([P, R_PASSES, 2 * M], U8, name="w4_sb", align_bytes=64)
        nc.sync.dma_start(w4_sb[:].bitcast(I32), w4_words.rearrange("a p c -> p a c").bitcast(I32))
        for q in range(4):
            nc.sync.dma_start(
                w4_plane[32 * q : 32 * q + 4, :, :].bitcast(I32),
                w4_scales[:, 4 * q : 4 * q + 4, :].rearrange("a r c -> r a c").bitcast(I32),
            )
        p1 = load_list("p1", pos1)
        p2 = load_list("p2", pos2)
        level_sb = keep.tile([P, M_TILES], F32, name="level_sb")
        with nc.allow_non_contiguous_dma(reason="one level for each partition and tile of rows"):
            nc.sync.dma_start(level_sb[:], level.rearrange("(m p) -> p m", p=P))
        d1 = [first_stage(1, t, PACK + t, whole) for t in range(PACK)]
        values = []
        for t in range(PACK):
            engine = nc.vector if t == 0 else nc.gpsimd
            values.append(weighted(engine, features(d1[t], 1, t), 1, t, f"values_slot{t}" if t else "weight_slot03"))
        for t in range(PACK):
            join(0, t)
        x_grouped = [group_x(0, half) for half in range(HALVES)]
        page_grouped = [group_page(0, half) for half in range(HALVES)]
        for t in range(PACK):
            scatter_values(values[t], 1, t)
            join(1, t)
        candidates = [gather_candidates(0, keep, "values_slot2", "values_slot1")]
        codes = keep.tile([P, 2 * HALVES, HALF], U32, name="second_codes0", tag="values_slot3", align_bytes=64)
        for half in range(HALVES):
            page_q[0, half] = quantise_into(f"page_q0{half}", codes[:, half, :], page_grouped[half])
        for half in range(HALVES):
            x_q[0, half] = quantise_into(f"x0{half}", codes[:, HALVES + half, :], x_grouped[half])
        x_grouped = [group_x(1, half) for half in range(HALVES)]
        page_grouped = [group_page(1, half) for half in range(HALVES)]
        for half in range(HALVES):
            page_q[1, half] = quantise(f"page_q1{half}", page_grouped[half])
            x_q[1, half] = quantise(f"x1{half}", x_grouped[half])
        candidates.append(gather_candidates(1, ring, "x_grouped", "x_grouped"))

        neg_level = keep.tile([P, M_TILES], F32, name="neg_level")
        nc.scalar.activation(neg_level[:], level_sb[:], ACT.Copy, scale=-1.0)

        e_banks = {(m, half): bank(HALVES * m + half, f"e{m}{half}") for m in range(M_TILES) for half in range(HALVES)}

        def second_stage(m, steps):
            for step, (product, b) in steps:
                for half in range(HALVES):
                    if product == "x":
                        lhs = w4_sb[:, b, 2 * m * P : 2 * (m + 1) * P].bitcast(FP4X4)
                        lhs_scale = w4_plane[:, b, m * P : (m + 1) * P]
                        codes, scales = x_q[b, half]
                    else:
                        words, planes = candidates[m // 2]
                        cols = slice(m % 2 * P, (m % 2 + 1) * P)
                        lhs = words[:, b, cols].bitcast(FP8X4)
                        lhs_scale = planes[4 * b :, cols]
                        codes, scales = page_q[b, half]
                    nc.tensor.matmul_mx(
                        out=e_banks[m, half][:], lhsT=lhs, lhsT_scale=lhs_scale,
                        rhs=codes.bitcast(FP8X4), rhs_scale=scales[:],
                        start=(step == 0), stop=(step == 2 * R_PASSES - 1),
                    )

        early = list(enumerate([("x", 0), ("page", 0), ("page", 1), ("x", 1)]))
        late = list(enumerate([("x", 0), ("x", 1), ("page", 0), ("page", 1)]))
        for m in range(M_TILES):
            second_stage(m, early if m < 2 else late)

        scores = []
        for m in range(M_TILES):
            e = keep.tile([P, T2], F32, name=f"scores{m}", tag=f"page_slot0{m}", align_bytes=64)
            for half in range(HALVES):
                nc.scalar.copy(e[:, half * HALF : (half + 1) * HALF], e_banks[m, half][:])
            scores.append(e)
        for m, e in enumerate(scores):
            seaward = keep.tile([P, S], F32, name=f"seaward{m}", tag=f"weight_slot0{m}", align_bytes=64)
            landward = keep.tile([P, S], F32, name=f"landward{m}", tag=f"root_slot{m}", align_bytes=64)
            nc.vector.tensor_copy(seaward[:], e[:].indirect(p1[:]))
            nc.vector.tensor_copy(landward[:], e[:].indirect(p2[:]))
            if m < 2:
                above = keep.tile([P, S], F32, name=f"above{m}", tag=f"page_q1{1 - m}_codes", align_bytes=64)
            else:
                above = ring.tile([P, S], F32, name=f"above{m}", tag="x_grouped", align_bytes=64)
            nc.scalar.activation(above[:], seaward[:], ACT.Identity, bias=neg_level[:, m : m + 1])
            result = keep.tile([P, S], F32, name=f"result{m}", tag=f"weight_slot1{m}", align_bytes=64)
            nc.vector.scalar_tensor_tensor(
                result[:], landward[:], level_sb[:, m : m + 1], above[:], ALU.subtract, ALU.max
            )
            nc.sync.dma_start(out[m * P : (m + 1) * P, :], result[:])
